import numpy as np
import ml_dtypes


def mxq(x, axis, fmt="e4m3"):
    dtype, down = {"e4m3": (ml_dtypes.float8_e4m3fn, 7), "e5m2": (ml_dtypes.float8_e5m2, 14)}[fmt]
    v = np.moveaxis(np.asarray(x, np.float32).astype(ml_dtypes.bfloat16).astype(np.float64), axis, -1)
    blocks = v.reshape(v.shape[:-1] + (-1, 32))
    amax = np.abs(blocks).max(-1, keepdims=True)
    byte = np.maximum(np.where(amax > 0, np.frexp(amax)[1] - 1 + 127, 0) - down, 1)
    scale = np.exp2(byte - 127.0)
    codes = (blocks / scale).astype(np.float32).astype(dtype).astype(np.float64)
    return np.moveaxis((codes * scale).reshape(v.shape), -1, axis)


WIDE = False


def mx_kscale(k):
    if not WIDE:
        return np.ones(k)
    levels = np.array([30, -30])
    if k % 512:
        return np.exp2(np.random.permutation(np.resize(levels, k // 32))).repeat(32)
    a = np.empty((k // 512, 16))
    for p in range(k // 512):
        a[p, :8] = np.random.permutation(np.resize(levels, 8))
        for g in range(8):
            far = levels[np.abs(levels - a[p, g]) >= 10]
            a[p, g + 8] = far[np.random.randint(len(far))]
    return np.exp2(a.ravel()).repeat(32)


BF16 = ml_dtypes.bfloat16


def bf(x):
    return np.asarray(x, np.float32).astype(BF16)


def f64(x):
    return np.asarray(x).astype(np.float64)


E2M1 = np.array([0.0, 0.5, 1.0, 1.5, 2.0, 3.0, 4.0, 6.0, -0.0, -0.5, -1.0, -1.5, -2.0, -3.0, -4.0, -6.0])


def pack_weight(w, fmt):
    k, n = w.shape
    w = f64(bf(w)).reshape(k // 32, 32, n)
    amax = np.abs(w).max(1)
    if fmt in ("e4m3", "e5m2"):
        byte = np.frexp(amax)[1] - 1 + 127 - (7 if fmt == "e4m3" else 14)
    else:
        mant, ex = np.frexp(amax / 6.0)
        byte = np.where(mant > 0.5, ex, ex - 1) + 127
    byte = np.clip(np.where(amax > 0, byte, 1), 1, 254)
    scaled = (w * np.exp2(127.0 - byte)[:, None, :]).reshape(k, n).astype(np.float32)
    by_word = np.ascontiguousarray(scaled.reshape(k // 512, 128, 4, n).transpose(0, 1, 3, 2))
    if fmt in ("e4m3", "e5m2"):
        words = by_word.astype(ml_dtypes.float8_e4m3fn if fmt == "e4m3" else ml_dtypes.float8_e5m2).view(np.uint8)
    else:
        c = by_word.astype(ml_dtypes.float4_e2m1fn).view(np.uint8) & 0xF
        words = c[..., 0::2] | (c[..., 1::2] << 4)
    return np.ascontiguousarray(words), np.ascontiguousarray(byte.astype(np.uint8).reshape(k // 512, 16, n))


def unpack_weight(words, scales, fmt):
    g, p, n, _ = words.shape
    if fmt in ("e4m3", "e5m2"):
        vals = np.ascontiguousarray(words).view(ml_dtypes.float8_e4m3fn if fmt == "e4m3" else ml_dtypes.float8_e5m2).astype(np.float64)
    else:
        nib = np.empty((g, p, n, 4), np.uint8)
        nib[..., 0::2] = words & 0xF
        nib[..., 1::2] = words >> 4
        vals = E2M1[nib]
    vals = vals * np.repeat(np.exp2(scales.astype(np.float64) - 127.0), 8, axis=1)[..., None]
    return vals.transpose(0, 1, 3, 2).reshape(g * 512, n)


S, P, F, R = 1024, 768, 1024, 512


def setup_inputs():
    s, t = mx_kscale(S), mx_kscale(R)
    G = np.random.standard_normal((S, 2 * F)) * np.exp(0.5 * np.random.standard_normal((S, 2 * F)))
    g_words, g_scales = pack_weight(G / s[:, None], "e5m2")
    return {"g_words": g_words, "g_scales": g_scales,
            "er": bf(np.random.standard_normal((S, P)) / np.sqrt(2 * S) * s[:, None]),
            "ei": bf(np.random.standard_normal((S, P)) / np.sqrt(2 * S) * s[:, None]),
            "ur": bf(np.random.standard_normal((P, R)) / np.sqrt(R) * t),
            "ui": bf(np.random.standard_normal((P, R)) / np.sqrt(R) * t),
            "v": bf(np.random.standard_normal((R, F)) / t[:, None])}


def reference(g_words, g_scales, er, ei, ur, ui, v):
    G = unpack_weight(g_words, g_scales, "e5m2")
    gr, gi = G[:, :F], G[:, F:]
    a = mxq(f64(er), 0, "e4m3").T
    b = mxq(f64(ei), 0, "e4m3").T
    vq = mxq(f64(v), 0, "e4m3")
    re = (a @ gr) + (b @ gi) + (mxq(f64(ur), 1, "e4m3") @ vq)
    im = (a @ gi) - (b @ gr) + (mxq(f64(ui), 1, "e4m3") @ vq)
    return re, im

@@ -1,0 +1,338 @@
+from contextlib import ExitStack
+
+import concourse.mybir as mybir
+
+F32 = mybir.dt.float32
+BF16 = mybir.dt.bfloat16
+U32 = mybir.dt.uint32
+I32 = mybir.dt.int32
+U8 = mybir.dt.uint8
+E4M3 = mybir.dt.float8_e4m3fn_x4
+E5M2 = mybir.dt.float8_e5m2_x4
+MULT = mybir.AluOpType.mult
+ADD = mybir.AluOpType.add
+COPY = mybir.ActivationFunctionType.Copy
+
+S, PIX, FR, R = 1024, 768, 1024, 512
+FLOPS = 2 * PIX * FR * (4 * S + 2 * R)
+
+P = 128
+HALF = 512
+PAIR = 256
+
+
+def tile_coil_adjoint_frame_update_e4_kernel(tc, g_words, g_scales, er, ei, ur, ui, v, out_0, out_1):
+    nc = tc.nc
+    with ExitStack() as ctx:
+        keep = ctx.enter_context(tc.tile_pool(name="keep", bufs=1))
+        stage = ctx.enter_context(tc.tile_pool(name="stage", bufs=1))
+        psum = ctx.enter_context(tc.psum_pool(name="psum", bufs=1))
+        ctx.enter_context(tc.manual_schedule())
+
+        def sb(shape, dtype, name):
+            return keep.tile(shape, dtype, name=name, align_bytes=256)
+
+        def staged(shape, dtype, tag, bufs):
+            return stage.tile(shape, dtype, name=tag, tag=tag, bufs=bufs, align_bytes=256)
+
+        enc = {"r": er, "i": ei}
+        spatial = {"r": ur, "i": ui}
+        outs = {"r": out_0, "i": out_1}
+
+        g_code = [sb([P, 4 * HALF], U32, "g_code%d" % g) for g in range(2)]
+        g_plane = sb([P, 2, 4 * HALF], U8, "g_plane")
+        plane_i32 = g_plane[:].rearrange("p g n -> p (g n)").bitcast(I32)
+        nc.vector.memset(plane_i32, 0)
+
+        raw_e = {}
+
+        def load_e(m, g, c0, w):
+            t = sb([P, 4, w], BF16, "raw_e%s%d_%d" % (m, g, c0))
+            src = enc[m][512 * g : 512 * (g + 1), c0 : c0 + w].rearrange("(p j) w -> p j w", j=4)
+            nc.sync.dma_start(out=t[:], in_=src)
+            for pair in range(c0 // PAIR, (c0 + w) // PAIR):
+                raw_e[m, g, pair] = (t, pair * PAIR - c0)
+
+        def load_g(g, c0, w=FR):
+            cols = slice(c0, c0 + w)
+            src = g_words[g].rearrange("p n t -> p (n t)")[:, 4 * c0 : 4 * (c0 + w)].bitcast(I32)
+            nc.sync.dma_start(out=g_code[g][:, cols].bitcast(I32), in_=src)
+
+        raw_u = {}
+
+        def load_u(m, b0, nb):
+            t = sb([P, nb, P], BF16, "raw_u%s_%d" % (m, b0))
+            src = spatial[m].rearrange("(b r) (q k) -> q r b k", r=32, k=P)
+            for q in range(4):
+                nc.sync.dma_start(out=t[32 * q : 32 * q + 32], in_=src[q, :, b0 : b0 + nb, :])
+            for pair in range(b0 // 8, (b0 + nb) // 8):
+                raw_u[m, pair] = (t, 8 * pair - b0)
+
+        raw_v = {}
+
+        def load_v(h):
+            t = sb([P, 4, HALF], BF16, "raw_v%d" % h)
+            nc.sync.dma_start(out=t[:], in_=v[:, HALF * h : HALF * (h + 1)].rearrange("(p j) f -> p j f", j=4))
+            raw_v[h] = t
+
+        load_e("r", 0, 0, PAIR)
+        for q in range(4):
+            nc.sync.dma_start(
+                out=g_plane[32 * q : 32 * q + 4].bitcast(I32),
+                in_=g_scales[:, 4 * q : 4 * q + 4, :].rearrange("g r n -> r g n").bitcast(I32),
+            )
+        load_e("i", 0, 0, PAIR)
+        load_g(0, 0, HALF)
+        load_g(0, HALF, HALF)
+        load_g(0, FR)
+        load_e("r", 1, 0, PAIR)
+        load_g(1, 0)
+        load_e("i", 1, 0, PAIR)
+        load_g(1, FR)
+        for g in range(2):
+            for m in "ri":
+                load_e(m, g, PAIR, PAIR)
+        load_v(0)
+        load_v(1)
+        for m in "ri":
+            load_u(m, 8, 8)
+        for g in range(2):
+            for m in "ri":
+                load_e(m, g, 2 * PAIR, PAIR)
+        for b0 in (16, 0):
+            for m in "ri":
+                load_u(m, b0, 8)
+
+        code = {}
+
+        def quantize(key, grouped, width):
+            c = sb([P, width], U32, "code_%s" % "_".join(str(k) for k in key))
+            s = sb([P, width], U8, "scale_%s" % "_".join(str(k) for k in key))
+            nc.vector.quantize_mx(out=c[:].bitcast(E4M3), scales=s[:], in_=grouped[:].rearrange("p w j -> p (w j)"))
+            code[key] = (c, s)
+
+        def make_e_split(m, g):
+            raw, off = raw_e[m, g, 0]
+            src = [raw[:, :, P * a : P * (a + 1)].rearrange("p j w -> p w j") for a in range(2)]
+            grp = [staged([P, P, 4], BF16, "grp_h", 4) for a in range(2)]
+            nc.vector.tensor_copy(out=grp[0][:], in_=src[0])
+            if m == "i":
+                neg = [staged([P, P, 4], BF16, "neg_h", 4) for a in range(2)]
+                nc.scalar.activation(out=neg[1][:], in_=src[1], func=COPY, scale=-1.0)
+                nc.vector.tensor_scalar(out=neg[0][:], in0=grp[0][:], scalar1=-1.0, scalar2=None, op0=MULT)
+            nc.scalar.copy(out=grp[1][:], in_=src[1])
+            if m == "i":
+                for a in range(2):
+                    quantize(("e", "n", g, a), neg[a], P)
+            for a in range(2):
+                quantize(("e", m, g, a), grp[a], P)
+
+        def make_e(g, pair, neg_on_vector):
+            grp = {}
+            for m in "ri":
+                raw, off = raw_e[m, g, pair]
+                grp[m] = staged([P, PAIR, 4], BF16, "grp_e", 4)
+                nc.vector.tensor_copy(out=grp[m][:], in_=raw[:].rearrange("p j w -> p w j"))
+            grp["n"] = staged([P, PAIR, 4], BF16, "neg_e", 2)
+            if not neg_on_vector:
+                nc.scalar.activation(out=grp["n"][:], in_=grp["i"][:], func=COPY, scale=-1.0)
+            quantize(("e", "r", g, pair, 0), grp["r"], PAIR)
+            if neg_on_vector:
+                nc.vector.tensor_scalar(out=grp["n"][:], in0=grp["i"][:], scalar1=-1.0, scalar2=None, op0=MULT)
+            quantize(("e", "i", g, pair, 0), grp["i"], PAIR)
+            quantize(("e", "n", g, pair, 0), grp["n"], PAIR)
+
+        perm_u = {}
+
+        def permute_u(pair):
+            for m in "ri":
+                raw, off = raw_u[m, pair]
+                t = staged([P, 8, 64], F32, "perm_u", 4)
+                words = raw[:].bitcast(F32)
+                nc.scalar.copy(
+                    out=t[:].rearrange("p b (u c) -> p b u c", u=2), in_=words.rearrange("p b (c u) -> p b u c", u=2)
+                )
+                perm_u[m, pair] = t
+
+        turned = {}
+        grouped_u = {}
+
+        def turn_u(pair):
+            for m in "ri":
+                t = staged([P, 512], F32, "turn_u", 4)
+                nc.vector.transpose(t[:], perm_u[m, pair][:].rearrange("p b w -> p (b w)"))
+                turned[m, pair] = t
+
+        def group_u(pair, copy):
+            for m in "ri":
+                gt = staged([P, PAIR, 4], BF16, "grp_u", 4)
+                copy(
+                    out=gt[:].rearrange("p w j -> p (w j)").bitcast(F32).rearrange("p (b r u) -> p b r u", b=8, u=2),
+                    in_=turned[m, pair][:].rearrange("p (b u r) -> p b r u", b=8, u=2),
+                )
+                grouped_u[m, pair] = gt
+
+        def quantize_u(pair):
+            for m in "ri":
+                quantize(("u", m, pair), grouped_u[m, pair], PAIR)
+
+        grp_v = {}
+
+        def group_v(h, copy):
+            grp_v[h] = staged([P, HALF, 4], BF16, "grp_v", 2)
+            copy(out=grp_v[h][:], in_=raw_v[h][:].rearrange("p j w -> p w j"))
+
+        bank = {}
+        done = {}
+        slots = [0]
+
+        def open_bank(key):
+            bank[key] = psum.tile([P, HALF], F32, name="bank%d" % (slots[0] % 8))
+            slots[0] += 1
+
+        def mx_u(i, h, c, start, stop):
+            lc, ls = code["u", c, i // 2]
+            cols = slice(P * (i % 2), P * (i % 2) + P)
+            rc, rs = code["v", h]
+            nc.tensor.matmul_mx(
+                out=bank[i, h, c][:],
+                lhsT=lc[:, cols].bitcast(E4M3),
+                lhsT_scale=ls[:, cols],
+                rhs=rc[:].bitcast(E4M3),
+                rhs_scale=rs[:],
+                start=start,
+                stop=stop,
+            )
+
+        def mx(i, h, c, m, g):
+            n = done.get((i, h, c), 0)
+            if n == 0:
+                open_bank((i, h, c))
+            if m == "r":
+                lm, part = "r", c
+            else:
+                lm, part = ("i", "i") if c == "r" else ("n", "r")
+            if i < 2:
+                lc, ls = code["e", lm, g, i]
+                cols = slice(0, P)
+            else:
+                lc, ls = code["e", lm, g, i // 2, 0]
+                cols = slice(P * (i % 2), P * (i % 2) + P)
+            n0 = (FR if part == "i" else 0) + HALF * h
+            nc.tensor.matmul_mx(
+                out=bank[i, h, c][:],
+                lhsT=lc[:, cols].bitcast(E4M3),
+                lhsT_scale=ls[:, cols],
+                rhs=g_code[g][:, n0 : n0 + HALF].bitcast(E5M2),
+                rhs_scale=g_plane[:, g, n0 : n0 + HALF],
+                start=(n == 0),
+                stop=(n == 3 and i < 2),
+            )
+            done[i, h, c] = n + 1
+
+        part = {}
+
+        def hold(i, h, c):
+            if h == 0:
+                part[i, c] = staged([P, FR], F32, "part", 4)
+            nc.scalar.copy(out=part[i, c][:, HALF * h : HALF * (h + 1)], in_=bank[i, h, c][:])
+
+        def add_u(i, h, c):
+            open_bank((i, h, c))
+            mx_u(i, h, c, True, True)
+            cols = slice(HALF * h, HALF * (h + 1))
+            t = part[i, c]
+            nc.vector.tensor_tensor(out=t[:, cols], in0=bank[i, h, c][:], in1=t[:, cols], op=ADD)
+            if h == 1:
+                nc.sync.dma_start(out=outs[c][P * i : P * (i + 1), :], in_=t[:])
+
+        result = {}
+
+        def finish(i, h, c, whole=True):
+            if h == 0:
+                result[i, c] = staged([P, FR], F32, "res", 6)
+            cols = slice(HALF * h, HALF * (h + 1))
+            res = result[i, c]
+            nc.scalar.copy(out=res[:, cols], in_=bank[i, h, c][:])
+            rows = slice(P * i, P * (i + 1))
+            if not whole:
+                nc.sync.dma_start(out=outs[c][rows, cols], in_=res[:, cols])
+            elif h == 1:
+                nc.sync.dma_start(out=outs[c][rows, :], in_=res[:])
+
+        groups01 = [(i, h) for i in (0, 1) for h in (0, 1)]
+
+        make_e_split("r", 0)
+        make_e_split("i", 0)
+        for h in (0, 1):
+            for i in (0, 1):
+                mx(i, h, "r", "r", 0)
+        for h in (0, 1):
+            for i in (0, 1):
+                mx(i, h, "i", "i", 0)
+        for i, h in groups01:
+            mx(i, h, "i", "r", 0)
+        for i, h in groups01:
+            mx(i, h, "r", "i", 0)
+        make_e_split("r", 1)
+        for i, h in groups01:
+            mx(i, h, "r", "r", 1)
+        make_e_split("i", 1)
+        for i, h in groups01:
+            mx(i, h, "r", "i", 1)
+            hold(i, h, "r")
+        for i, h in groups01:
+            mx(i, h, "i", "i", 1)
+            mx(i, h, "i", "r", 1)
+            hold(i, h, "i")
+
+        groups23 = [(i, c, h) for h in (0, 1) for i in (2, 3) for c in "ri"]
+        make_e(0, 1, True)
+        for m in "ri":
+            for i, c, h in groups23:
+                mx(i, h, c, m, 0)
+        make_e(1, 1, True)
+        for i, c, h in groups23:
+            mx(i, h, c, "r", 1)
+        permute_u(1)
+        group_v(1, nc.scalar.copy)
+        group_v(0, nc.vector.tensor_copy)
+        turn_u(1)
+        quantize(("v", 0), grp_v[0], HALF)
+        group_u(1, nc.vector.tensor_copy)
+        quantize_u(1)
+        quantize(("v", 1), grp_v[1], HALF)
+        for i, c, h in groups23:
+            mx(i, h, c, "i", 1)
+            mx_u(i, h, c, False, True)
+            finish(i, h, c)
+
+        make_e(0, 2, True)
+        make_e(1, 2, True)
+        permute_u(2)
+        turn_u(2)
+        group_u(2, nc.vector.tensor_copy)
+        quantize_u(2)
+        permute_u(0)
+        turn_u(0)
+        group_u(0, nc.scalar.copy)
+        quantize_u(0)
+        late = [(i, c, h) for i in (0, 1) for c in "ri" for h in (0, 1)]
+        groups45 = [(i, c, h) for i in (4, 5) for c in "ri" for h in (0, 1)]
+
+        def last(n, whole=True):
+            i, c, h = groups45[n]
+            mx_u(i, h, c, False, True)
+            finish(i, h, c, whole)
+
+        for n, (i, c, h) in enumerate(groups45):
+            for g in range(2):
+                for m in "ri":
+                    mx(i, h, c, m, g)
+            if n == 1:
+                last(0)
+            if n >= 1:
+                last(n, n < 6)
+            if 2 <= n < 6:
+                for j, d, k in late[2 * n - 4 : 2 * n - 2]:
+                    add_u(j, k, d)

@@ -19,6 +19,7 @@ FLOPS = 2 * PIX * FR * (4 * S + 2 * R)
 P = 128
 HALF = 512
 PAIR = 256
+WARM = 16
 
 
 def tile_coil_adjoint_frame_update_e4_kernel(tc, g_words, g_scales, er, ei, ur, ui, v, out_0, out_1):
@@ -43,6 +44,25 @@ def tile_coil_adjoint_frame_update_e4_kernel(tc, g_words, g_scales, er, ei, ur, 
         g_plane = sb([P, 2, 4 * HALF], U8, "g_plane")
         plane_i32 = g_plane[:].rearrange("p g n -> p (g n)").bitcast(I32)
         nc.vector.memset(plane_i32, 0)
+
+        warm_grp = sb([P, PAIR, 4], BF16, "warm_grp")
+        warm_code = sb([P, PAIR], U32, "warm_code")
+        warm_scale = sb([P, PAIR], U8, "warm_scale")
+        nc.vector.memset(warm_grp[:].rearrange("p w j -> p (w j)").bitcast(I32), 0)
+        nc.vector.quantize_mx(
+            out=warm_code[:].bitcast(E4M3), scales=warm_scale[:], in_=warm_grp[:].rearrange("p w j -> p (w j)")
+        )
+        warm_bank = psum.tile([P, HALF], F32, name="bank7")
+        for n in range(WARM):
+            nc.tensor.matmul_mx(
+                out=warm_bank[:, :PAIR],
+                lhsT=warm_code[:, :P].bitcast(E4M3),
+                lhsT_scale=warm_scale[:, :P],
+                rhs=warm_code[:].bitcast(E4M3),
+                rhs_scale=warm_scale[:],
+                start=True,
+                stop=True,
+            )
 
         raw_e = {}
 
@@ -140,7 +160,9 @@ def tile_coil_adjoint_frame_update_e4_kernel(tc, g_words, g_scales, er, ei, ur, 
             if neg_on_vector:
                 nc.vector.tensor_scalar(out=grp["n"][:], in0=grp["i"][:], scalar1=-1.0, scalar2=None, op0=MULT)
             quantize(("e", "i", g, pair, 0), grp["i"], PAIR)
-            quantize(("e", "n", g, pair, 0), grp["n"], PAIR)
+            if neg_on_vector:
+                quantize(("e", "n", g, pair, 0), grp["n"], PAIR)
+            return grp["n"]
 
         perm_u = {}
 
@@ -291,48 +313,58 @@ def tile_coil_adjoint_frame_update_e4_kernel(tc, g_words, g_scales, er, ei, ur, 
         for m in "ri":
             for i, c, h in groups23:
                 mx(i, h, c, m, 0)
-        make_e(1, 1, True)
+        neg = make_e(1, 1, False)
+        quantize_neg = lambda: quantize(("e", "n", 1, 1, 0), neg, PAIR)
         for i, c, h in groups23:
             mx(i, h, c, "r", 1)
         permute_u(1)
         group_v(1, nc.scalar.copy)
         group_v(0, nc.vector.tensor_copy)
+        quantize_neg()
         turn_u(1)
         quantize(("v", 0), grp_v[0], HALF)
         group_u(1, nc.vector.tensor_copy)
         quantize_u(1)
         quantize(("v", 1), grp_v[1], HALF)
-        for i, c, h in groups23:
-            mx(i, h, c, "i", 1)
-            mx_u(i, h, c, False, True)
-            finish(i, h, c)
 
+        def close(i, c, h, whole=True):
+            mx_u(i, h, c, False, True)
+            finish(i, h, c, whole)
+
+        LAG = 2
+        for n in range(8 + LAG):
+            if n < 8:
+                i, c, h = groups23[n]
+                mx(i, h, c, "i", 1)
+            if n >= LAG:
+                close(*groups23[n - LAG])
+
+        groups45 = [(i, c, h) for i in (4, 5) for c in "ri" for h in (0, 1)]
         make_e(0, 2, True)
+        for m in "ri":
+            for i, c, h in groups45[:4]:
+                mx(i, h, c, m, 0)
         make_e(1, 2, True)
+        for m in "ri":
+            for i, c, h in groups45[:4]:
+                mx(i, h, c, m, 1)
         permute_u(2)
         turn_u(2)
         group_u(2, nc.vector.tensor_copy)
         quantize_u(2)
         permute_u(0)
         turn_u(0)
-        group_u(0, nc.scalar.copy)
+        group_u(0, nc.vector.tensor_copy)
         quantize_u(0)
+        for n in range(4):
+            close(*groups45[n])
         late = [(i, c, h) for i in (0, 1) for c in "ri" for h in (0, 1)]
-        groups45 = [(i, c, h) for i in (4, 5) for c in "ri" for h in (0, 1)]
-
-        def last(n, whole=True):
+        for n in range(4, 8):
             i, c, h = groups45[n]
-            mx_u(i, h, c, False, True)
-            finish(i, h, c, whole)
-
-        for n, (i, c, h) in enumerate(groups45):
             for g in range(2):
                 for m in "ri":
                     mx(i, h, c, m, g)
-            if n == 1:
-                last(0)
-            if n >= 1:
-                last(n, n < 6)
-            if 2 <= n < 6:
-                for j, d, k in late[2 * n - 4 : 2 * n - 2]:
-                    add_u(j, k, d)
+            close(i, c, h, n < 6)
+            for j, d, k in late[: (4, 4, 0, 0)[n - 4]]:
+                add_u(j, k, d)
+                late.pop(0)

@@ -19,7 +19,7 @@ FLOPS = 2 * PIX * FR * (4 * S + 2 * R)
 P = 128
 HALF = 512
 PAIR = 256
-WARM = 16
+WARM = 13
 
 
 def tile_coil_adjoint_frame_update_e4_kernel(tc, g_words, g_scales, er, ei, ur, ui, v, out_0, out_1):
@@ -43,7 +43,7 @@ def tile_coil_adjoint_frame_update_e4_kernel(tc, g_words, g_scales, er, ei, ur, 
         g_code = [sb([P, 4 * HALF], U32, "g_code%d" % g) for g in range(2)]
         g_plane = sb([P, 2, 4 * HALF], U8, "g_plane")
         plane_i32 = g_plane[:].rearrange("p g n -> p (g n)").bitcast(I32)
-        nc.vector.memset(plane_i32, 0)
+        nc.gpsimd.memset(plane_i32, 0)
 
         warm_grp = sb([P, PAIR, 4], BF16, "warm_grp")
         warm_code = sb([P, PAIR], U32, "warm_code")
@@ -96,26 +96,26 @@ def tile_coil_adjoint_frame_update_e4_kernel(tc, g_words, g_scales, er, ei, ur, 
             raw_v[h] = t
 
         load_e("r", 0, 0, PAIR)
+        load_e("i", 0, 0, PAIR)
         for q in range(4):
             nc.sync.dma_start(
                 out=g_plane[32 * q : 32 * q + 4].bitcast(I32),
                 in_=g_scales[:, 4 * q : 4 * q + 4, :].rearrange("g r n -> r g n").bitcast(I32),
             )
-        load_e("i", 0, 0, PAIR)
         load_g(0, 0, HALF)
         load_g(0, HALF, HALF)
         load_g(0, FR)
         load_e("r", 1, 0, PAIR)
-        load_g(1, 0)
         load_e("i", 1, 0, PAIR)
+        load_g(1, 0)
         load_g(1, FR)
         for g in range(2):
             for m in "ri":
                 load_e(m, g, PAIR, PAIR)
         load_v(0)
-        load_v(1)
         for m in "ri":
             load_u(m, 8, 8)
+        load_v(1)
         for g in range(2):
             for m in "ri":
                 load_e(m, g, 2 * PAIR, PAIR)
@@ -270,16 +270,18 @@ def tile_coil_adjoint_frame_update_e4_kernel(tc, g_words, g_scales, er, ei, ur, 
 
         result = {}
 
-        def finish(i, h, c, whole=True):
+        def finish(i, h, c, pieces=0):
             if h == 0:
                 result[i, c] = staged([P, FR], F32, "res", 6)
-            cols = slice(HALF * h, HALF * (h + 1))
             res = result[i, c]
-            nc.scalar.copy(out=res[:, cols], in_=bank[i, h, c][:])
             rows = slice(P * i, P * (i + 1))
-            if not whole:
-                nc.sync.dma_start(out=outs[c][rows, cols], in_=res[:, cols])
-            elif h == 1:
+            w = HALF // max(pieces, 1)
+            for k in range(max(pieces, 1)):
+                cols = slice(HALF * h + w * k, HALF * h + w * (k + 1))
+                nc.scalar.copy(out=res[:, cols], in_=bank[i, h, c][:, w * k : w * (k + 1)])
+                if pieces:
+                    nc.sync.dma_start(out=outs[c][rows, cols], in_=res[:, cols])
+            if h == 1 and not pieces:
                 nc.sync.dma_start(out=outs[c][rows, :], in_=res[:])
 
         groups01 = [(i, h) for i in (0, 1) for h in (0, 1)]
@@ -327,9 +329,9 @@ def tile_coil_adjoint_frame_update_e4_kernel(tc, g_words, g_scales, er, ei, ur, 
         quantize_u(1)
         quantize(("v", 1), grp_v[1], HALF)
 
-        def close(i, c, h, whole=True):
+        def close(i, c, h, pieces=0):
             mx_u(i, h, c, False, True)
-            finish(i, h, c, whole)
+            finish(i, h, c, pieces)
 
         LAG = 2
         for n in range(8 + LAG):
@@ -364,7 +366,7 @@ def tile_coil_adjoint_frame_update_e4_kernel(tc, g_words, g_scales, er, ei, ur, 
             for g in range(2):
                 for m in "ri":
                     mx(i, h, c, m, g)
-            close(i, c, h, n < 6)
+            close(i, c, h, (0, 0, 1, 2)[n - 4])
             for j, d, k in late[: (4, 4, 0, 0)[n - 4]]:
                 add_u(j, k, d)
                 late.pop(0)

from contextlib import ExitStack

import concourse.mybir as mybir

F32 = mybir.dt.float32
BF16 = mybir.dt.bfloat16
U32 = mybir.dt.uint32
I32 = mybir.dt.int32
U8 = mybir.dt.uint8
E4M3 = mybir.dt.float8_e4m3fn_x4
E5M2 = mybir.dt.float8_e5m2_x4
MULT = mybir.AluOpType.mult
ADD = mybir.AluOpType.add
COPY = mybir.ActivationFunctionType.Copy

S, PIX, FR, R = 1024, 768, 1024, 512
FLOPS = 2 * PIX * FR * (4 * S + 2 * R)

P = 128
HALF = 512
PAIR = 256
WARM = 13


def tile_coil_adjoint_frame_update_e4_kernel(tc, g_words, g_scales, er, ei, ur, ui, v, out_0, out_1):
    nc = tc.nc
    with ExitStack() as ctx:
        keep = ctx.enter_context(tc.tile_pool(name="keep", bufs=1))
        stage = ctx.enter_context(tc.tile_pool(name="stage", bufs=1))
        psum = ctx.enter_context(tc.psum_pool(name="psum", bufs=1))
        ctx.enter_context(tc.manual_schedule())

        def sb(shape, dtype, name):
            return keep.tile(shape, dtype, name=name, align_bytes=256)

        def staged(shape, dtype, tag, bufs):
            return stage.tile(shape, dtype, name=tag, tag=tag, bufs=bufs, align_bytes=256)

        enc = {"r": er, "i": ei}
        spatial = {"r": ur, "i": ui}
        outs = {"r": out_0, "i": out_1}

        g_code = [sb([P, 4 * HALF], U32, "g_code%d" % g) for g in range(2)]
        g_plane = sb([P, 2, 4 * HALF], U8, "g_plane")
        plane_i32 = g_plane[:].rearrange("p g n -> p (g n)").bitcast(I32)
        nc.gpsimd.memset(plane_i32, 0)

        warm_grp = sb([P, PAIR, 4], BF16, "warm_grp")
        warm_code = sb([P, PAIR], U32, "warm_code")
        warm_scale = sb([P, PAIR], U8, "warm_scale")
        nc.vector.memset(warm_grp[:].rearrange("p w j -> p (w j)").bitcast(I32), 0)
        nc.vector.quantize_mx(
            out=warm_code[:].bitcast(E4M3), scales=warm_scale[:], in_=warm_grp[:].rearrange("p w j -> p (w j)")
        )
        warm_bank = psum.tile([P, HALF], F32, name="bank7")
        for n in range(WARM):
            nc.tensor.matmul_mx(
                out=warm_bank[:, :PAIR],
                lhsT=warm_code[:, :P].bitcast(E4M3),
                lhsT_scale=warm_scale[:, :P],
                rhs=warm_code[:].bitcast(E4M3),
                rhs_scale=warm_scale[:],
                start=True,
                stop=True,
            )

        raw_e = {}

        def load_e(m, g, c0, w):
            t = sb([P, 4, w], BF16, "raw_e%s%d_%d" % (m, g, c0))
            src = enc[m][512 * g : 512 * (g + 1), c0 : c0 + w].rearrange("(p j) w -> p j w", j=4)
            nc.sync.dma_start(out=t[:], in_=src)
            for pair in range(c0 // PAIR, (c0 + w) // PAIR):
                raw_e[m, g, pair] = (t, pair * PAIR - c0)

        def load_g(g, c0, w=FR):
            cols = slice(c0, c0 + w)
            src = g_words[g].rearrange("p n t -> p (n t)")[:, 4 * c0 : 4 * (c0 + w)].bitcast(I32)
            nc.sync.dma_start(out=g_code[g][:, cols].bitcast(I32), in_=src)

        raw_u = {}

        def load_u(m, b0, nb):
            t = sb([P, nb, P], BF16, "raw_u%s_%d" % (m, b0))
            src = spatial[m].rearrange("(b r) (q k) -> q r b k", r=32, k=P)
            for q in range(4):
                nc.sync.dma_start(out=t[32 * q : 32 * q + 32], in_=src[q, :, b0 : b0 + nb, :])
            for pair in range(b0 // 8, (b0 + nb) // 8):
                raw_u[m, pair] = (t, 8 * pair - b0)

        raw_v = {}

        def load_v(h):
            t = sb([P, 4, HALF], BF16, "raw_v%d" % h)
            nc.sync.dma_start(out=t[:], in_=v[:, HALF * h : HALF * (h + 1)].rearrange("(p j) f -> p j f", j=4))
            raw_v[h] = t

        load_e("r", 0, 0, PAIR)
        load_e("i", 0, 0, PAIR)
        for q in range(4):
            nc.sync.dma_start(
                out=g_plane[32 * q : 32 * q + 4].bitcast(I32),
                in_=g_scales[:, 4 * q : 4 * q + 4, :].rearrange("g r n -> r g n").bitcast(I32),
            )
        load_g(0, 0, HALF)
        load_g(0, HALF, HALF)
        load_g(0, FR)
        load_e("r", 1, 0, PAIR)
        load_e("i", 1, 0, PAIR)
        load_g(1, 0)
        load_g(1, FR)
        for g in range(2):
            for m in "ri":
                load_e(m, g, PAIR, PAIR)
        load_v(0)
        for m in "ri":
            load_u(m, 8, 8)
        load_v(1)
        for g in range(2):
            for m in "ri":
                load_e(m, g, 2 * PAIR, PAIR)
        for b0 in (16, 0):
            for m in "ri":
                load_u(m, b0, 8)

        code = {}

        def quantize(key, grouped, width):
            c = sb([P, width], U32, "code_%s" % "_".join(str(k) for k in key))
            s = sb([P, width], U8, "scale_%s" % "_".join(str(k) for k in key))
            nc.vector.quantize_mx(out=c[:].bitcast(E4M3), scales=s[:], in_=grouped[:].rearrange("p w j -> p (w j)"))
            code[key] = (c, s)

        def make_e_split(m, g):
            raw, off = raw_e[m, g, 0]
            src = [raw[:, :, P * a : P * (a + 1)].rearrange("p j w -> p w j") for a in range(2)]
            grp = [staged([P, P, 4], BF16, "grp_h", 4) for a in range(2)]
            nc.vector.tensor_copy(out=grp[0][:], in_=src[0])
            if m == "i":
                neg = [staged([P, P, 4], BF16, "neg_h", 4) for a in range(2)]
                nc.scalar.activation(out=neg[1][:], in_=src[1], func=COPY, scale=-1.0)
                nc.vector.tensor_scalar(out=neg[0][:], in0=grp[0][:], scalar1=-1.0, scalar2=None, op0=MULT)
            nc.scalar.copy(out=grp[1][:], in_=src[1])
            if m == "i":
                for a in range(2):
                    quantize(("e", "n", g, a), neg[a], P)
            for a in range(2):
                quantize(("e", m, g, a), grp[a], P)

        def make_e(g, pair, neg_on_vector):
            grp = {}
            for m in "ri":
                raw, off = raw_e[m, g, pair]
                grp[m] = staged([P, PAIR, 4], BF16, "grp_e", 4)
                nc.vector.tensor_copy(out=grp[m][:], in_=raw[:].rearrange("p j w -> p w j"))
            grp["n"] = staged([P, PAIR, 4], BF16, "neg_e", 2)
            if not neg_on_vector:
                nc.scalar.activation(out=grp["n"][:], in_=grp["i"][:], func=COPY, scale=-1.0)
            quantize(("e", "r", g, pair, 0), grp["r"], PAIR)
            if neg_on_vector:
                nc.vector.tensor_scalar(out=grp["n"][:], in0=grp["i"][:], scalar1=-1.0, scalar2=None, op0=MULT)
            quantize(("e", "i", g, pair, 0), grp["i"], PAIR)
            if neg_on_vector:
                quantize(("e", "n", g, pair, 0), grp["n"], PAIR)
            return grp["n"]

        perm_u = {}

        def permute_u(pair):
            for m in "ri":
                raw, off = raw_u[m, pair]
                t = staged([P, 8, 64], F32, "perm_u", 4)
                words = raw[:].bitcast(F32)
                nc.scalar.copy(
                    out=t[:].rearrange("p b (u c) -> p b u c", u=2), in_=words.rearrange("p b (c u) -> p b u c", u=2)
                )
                perm_u[m, pair] = t

        turned = {}
        grouped_u = {}

        def turn_u(pair):
            for m in "ri":
                t = staged([P, 512], F32, "turn_u", 4)
                nc.vector.transpose(t[:], perm_u[m, pair][:].rearrange("p b w -> p (b w)"))
                turned[m, pair] = t

        def group_u(pair, copy):
            for m in "ri":
                gt = staged([P, PAIR, 4], BF16, "grp_u", 4)
                copy(
                    out=gt[:].rearrange("p w j -> p (w j)").bitcast(F32).rearrange("p (b r u) -> p b r u", b=8, u=2),
                    in_=turned[m, pair][:].rearrange("p (b u r) -> p b r u", b=8, u=2),
                )
                grouped_u[m, pair] = gt

        def quantize_u(pair):
            for m in "ri":
                quantize(("u", m, pair), grouped_u[m, pair], PAIR)

        grp_v = {}

        def group_v(h, copy):
            grp_v[h] = staged([P, HALF, 4], BF16, "grp_v", 2)
            copy(out=grp_v[h][:], in_=raw_v[h][:].rearrange("p j w -> p w j"))

        bank = {}
        done = {}
        slots = [0]

        def open_bank(key):
            bank[key] = psum.tile([P, HALF], F32, name="bank%d" % (slots[0] % 8))
            slots[0] += 1

        def mx_u(i, h, c, start, stop):
            lc, ls = code["u", c, i // 2]
            cols = slice(P * (i % 2), P * (i % 2) + P)
            rc, rs = code["v", h]
            nc.tensor.matmul_mx(
                out=bank[i, h, c][:],
                lhsT=lc[:, cols].bitcast(E4M3),
                lhsT_scale=ls[:, cols],
                rhs=rc[:].bitcast(E4M3),
                rhs_scale=rs[:],
                start=start,
                stop=stop,
            )

        def mx(i, h, c, m, g):
            n = done.get((i, h, c), 0)
            if n == 0:
                open_bank((i, h, c))
            if m == "r":
                lm, part = "r", c
            else:
                lm, part = ("i", "i") if c == "r" else ("n", "r")
            if i < 2:
                lc, ls = code["e", lm, g, i]
                cols = slice(0, P)
            else:
                lc, ls = code["e", lm, g, i // 2, 0]
                cols = slice(P * (i % 2), P * (i % 2) + P)
            n0 = (FR if part == "i" else 0) + HALF * h
            nc.tensor.matmul_mx(
                out=bank[i, h, c][:],
                lhsT=lc[:, cols].bitcast(E4M3),
                lhsT_scale=ls[:, cols],
                rhs=g_code[g][:, n0 : n0 + HALF].bitcast(E5M2),
                rhs_scale=g_plane[:, g, n0 : n0 + HALF],
                start=(n == 0),
                stop=(n == 3 and i < 2),
            )
            done[i, h, c] = n + 1

        part = {}

        def hold(i, h, c):
            if h == 0:
                part[i, c] = staged([P, FR], F32, "part", 4)
            nc.scalar.copy(out=part[i, c][:, HALF * h : HALF * (h + 1)], in_=bank[i, h, c][:])

        def add_u(i, h, c):
            open_bank((i, h, c))
            mx_u(i, h, c, True, True)
            cols = slice(HALF * h, HALF * (h + 1))
            t = part[i, c]
            nc.vector.tensor_tensor(out=t[:, cols], in0=bank[i, h, c][:], in1=t[:, cols], op=ADD)
            if h == 1:
                nc.sync.dma_start(out=outs[c][P * i : P * (i + 1), :], in_=t[:])

        result = {}

        def finish(i, h, c, pieces=0):
            if h == 0:
                result[i, c] = staged([P, FR], F32, "res", 6)
            res = result[i, c]
            rows = slice(P * i, P * (i + 1))
            w = HALF // max(pieces, 1)
            for k in range(max(pieces, 1)):
                cols = slice(HALF * h + w * k, HALF * h + w * (k + 1))
                nc.scalar.copy(out=res[:, cols], in_=bank[i, h, c][:, w * k : w * (k + 1)])
                if pieces:
                    nc.sync.dma_start(out=outs[c][rows, cols], in_=res[:, cols])
            if h == 1 and not pieces:
                nc.sync.dma_start(out=outs[c][rows, :], in_=res[:])

        groups01 = [(i, h) for i in (0, 1) for h in (0, 1)]

        make_e_split("r", 0)
        make_e_split("i", 0)
        for h in (0, 1):
            for i in (0, 1):
                mx(i, h, "r", "r", 0)
        for h in (0, 1):
            for i in (0, 1):
                mx(i, h, "i", "i", 0)
        for i, h in groups01:
            mx(i, h, "i", "r", 0)
        for i, h in groups01:
            mx(i, h, "r", "i", 0)
        make_e_split("r", 1)
        for i, h in groups01:
            mx(i, h, "r", "r", 1)
        make_e_split("i", 1)
        for i, h in groups01:
            mx(i, h, "r", "i", 1)
            hold(i, h, "r")
        for i, h in groups01:
            mx(i, h, "i", "i", 1)
            mx(i, h, "i", "r", 1)
            hold(i, h, "i")

        groups23 = [(i, c, h) for h in (0, 1) for i in (2, 3) for c in "ri"]
        make_e(0, 1, True)
        for m in "ri":
            for i, c, h in groups23:
                mx(i, h, c, m, 0)
        neg = make_e(1, 1, False)
        quantize_neg = lambda: quantize(("e", "n", 1, 1, 0), neg, PAIR)
        for i, c, h in groups23:
            mx(i, h, c, "r", 1)
        permute_u(1)
        group_v(1, nc.scalar.copy)
        group_v(0, nc.vector.tensor_copy)
        quantize_neg()
        turn_u(1)
        quantize(("v", 0), grp_v[0], HALF)
        group_u(1, nc.vector.tensor_copy)
        quantize_u(1)
        quantize(("v", 1), grp_v[1], HALF)

        def close(i, c, h, pieces=0):
            mx_u(i, h, c, False, True)
            finish(i, h, c, pieces)

        LAG = 2
        for n in range(8 + LAG):
            if n < 8:
                i, c, h = groups23[n]
                mx(i, h, c, "i", 1)
            if n >= LAG:
                close(*groups23[n - LAG])

        groups45 = [(i, c, h) for i in (4, 5) for c in "ri" for h in (0, 1)]
        make_e(0, 2, True)
        for m in "ri":
            for i, c, h in groups45[:4]:
                mx(i, h, c, m, 0)
        make_e(1, 2, True)
        for m in "ri":
            for i, c, h in groups45[:4]:
                mx(i, h, c, m, 1)
        permute_u(2)
        turn_u(2)
        group_u(2, nc.vector.tensor_copy)
        quantize_u(2)
        permute_u(0)
        turn_u(0)
        group_u(0, nc.vector.tensor_copy)
        quantize_u(0)
        for n in range(4):
            close(*groups45[n])
        late = [(i, c, h) for i in (0, 1) for c in "ri" for h in (0, 1)]
        for n in range(4, 8):
            i, c, h = groups45[n]
            for g in range(2):
                for m in "ri":
                    mx(i, h, c, m, g)
            close(i, c, h, (0, 0, 1, 2)[n - 4])
            for j, d, k in late[: (4, 4, 0, 0)[n - 4]]:
                add_u(j, k, d)
                late.pop(0)
